import numpy as np
import ml_dtypes


def mxq(x, axis, fmt="e4m3"):
    dtype, down = {"e4m3": (ml_dtypes.float8_e4m3fn, 7), "e5m2": (ml_dtypes.float8_e5m2, 14)}[fmt]
    v = np.moveaxis(np.asarray(x, np.float32).astype(ml_dtypes.bfloat16).astype(np.float64), axis, -1)
    blocks = v.reshape(v.shape[:-1] + (-1, 32))
    amax = np.abs(blocks).max(-1, keepdims=True)
    byte = np.maximum(np.where(amax > 0, np.frexp(amax)[1] - 1 + 127, 0) - down, 1)
    scale = np.exp2(byte - 127.0)
    codes = (blocks / scale).astype(np.float32).astype(dtype).astype(np.float64)
    return np.moveaxis((codes * scale).reshape(v.shape), -1, axis)


WIDE = False


def mx_kscale(k):
    if not WIDE:
        return np.ones(k)
    levels = np.array([10, -10, 5, -5, 0])
    if k % 512:
        return np.exp2(np.random.permutation(np.resize(levels, k // 32))).repeat(32)
    a = np.empty((k // 512, 16))
    for p in range(k // 512):
        a[p, :8] = np.random.permutation(np.resize(levels, 8))
        for g in range(8):
            far = levels[np.abs(levels - a[p, g]) >= 10]
            a[p, g + 8] = far[np.random.randint(len(far))]
    return np.exp2(a.ravel()).repeat(32)


def f64(x):
    return np.asarray(x).astype(np.float64)


def striped(idx):
    return np.tile(idx.reshape(-1, 16).T, (8, 1)).astype(np.uint16)


def unstriped(offs):
    return offs[:16].T.reshape(-1).astype(np.int64)


def relu2(v):
    return np.maximum(v, 0.0) ** 2


K, T, E, C, H, N = 2048, 768, 6, 128, 512, 384


def by_expert(wq, xq):
    return np.concatenate([wq[e].T @ xq[:, e * C:(e + 1) * C] for e in range(E)], axis=1)


def setup_inputs():
    n = np.random.standard_normal
    s = mx_kscale(K)[:, None]
    u = mx_kscale(H)
    return {
        "xT": (n((K, T)) * s).astype(np.float32),
        "w1": (n((E, K, H)) / np.sqrt(K) / s[None] * u[None, None, :]).astype(np.float32),
        "w2": (n((E, H, N)) / np.sqrt(H) / u[None, :, None] ** 2).astype(np.float32),
        "gate": np.tile(np.random.uniform(0.2, 1.0, E * C), (N, 1)).astype(np.float32),
        "offs": striped(np.random.permutation(T)[:E * C]),
    }


def reference(xT, w1, w2, gate, offs):
    idx = unstriped(offs)
    xq = mxq(f64(xT)[:, idx], 0, "e4m3")
    h = relu2(by_expert(mxq(f64(w1), 1, "e4m3"), xq))
    y = by_expert(mxq(f64(w2), 1, "e4m3"), mxq(h, 0, "e4m3"))
    out = np.zeros((N, T))
    out[:, idx] = f64(gate) * y
    return out

@@ -1,0 +1,236 @@
+from contextlib import ExitStack
+
+import concourse.mybir as mybir
+
+K, T, E, C, H, N = 2048, 768, 6, 128, 512, 384
+P = 128
+PACK = 4
+K_PASS = P * PACK
+PASSES = K // K_PASS
+NB = N // P
+SLOTS = E * C
+FLOPS = 2 * SLOTS * (K * H + H * N)
+
+F32 = mybir.dt.float32
+BF16 = mybir.dt.bfloat16
+U32 = mybir.dt.uint32
+U16 = mybir.dt.uint16
+U8 = mybir.dt.uint8
+FP8X4 = mybir.dt.float8_e4m3fn_x4
+RELU = mybir.ActivationFunctionType.Relu
+SQUARE = mybir.ActivationFunctionType.Square
+MULT = mybir.AluOpType.mult
+MAX = mybir.AluOpType.max
+
+X_VEC = 128
+W1_VEC = 32
+W2_VEC = 96
+HALF = SLOTS // 2
+GROUPS = [(0, 1), (2, 3), (4,), (5,)]
+
+
+def tile_routed_moe_kernel(tc, xT, w1, w2, gate, offs, out):
+    nc = tc.nc
+    with ExitStack() as ctx:
+        keep = ctx.enter_context(tc.tile_pool(name="keep", bufs=1))
+        rawp = ctx.enter_context(tc.tile_pool(name="rawp", bufs=6))
+        grp = ctx.enter_context(tc.tile_pool(name="grp", bufs=3))
+        wcp = ctx.enter_context(tc.tile_pool(name="wcp", bufs=6))
+        w2cp = ctx.enter_context(tc.tile_pool(name="w2cp", bufs=2))
+        hp = ctx.enter_context(tc.tile_pool(name="hp", bufs=2))
+        accp = ctx.enter_context(tc.psum_pool(name="accp", bufs=2))
+        yp = ctx.enter_context(tc.psum_pool(name="yp", bufs=2))
+        lastp = ctx.enter_context(tc.psum_pool(name="lastp", bufs=1))
+
+        offs_t = keep.tile([P, SLOTS // 16], U16, name="offs_t")
+        nc.sync.dma_start(offs_t[:], offs)
+        planes = keep.tile([P, T], U8, name="planes", align_bytes=64)
+        nc.gpsimd.memset(planes[:], 0)
+        planes_g = keep.tile([P, SLOTS], U8, name="planes_g", align_bytes=64)
+        gate_t = keep.tile([P, NB, SLOTS], F32, name="gate_t")
+        windows = [keep.tile([P, T], F32, name="window%d" % b) for b in range(NB)]
+        words = [keep.tile([P, T], U32, name="words%d" % s, align_bytes=64) for s in range(PASSES)]
+        words_g = [keep.tile([P, SLOTS], U32, name="words_g%d" % s, align_bytes=64) for s in range(PASSES)]
+        w1_codes = {}
+        w2_codes = {}
+        accs = {}
+        hidden = {}
+        ys = {}
+
+        def slots(e, n=1):
+            return slice(e * C, (e + n) * C)
+
+        def gather(dst, src):
+            for lo in (0, HALF):
+                nc.vector.tensor_copy(dst[:, lo : lo + HALF], src[:].indirect(offs_t[:, lo // 16 : (lo + HALF) // 16]))
+
+        def quantize(codes, scales, flat, width):
+            lo = 0
+            while lo < width:
+                hi = lo + max(w for w in (1024, 512, 256, 128) if w <= width - lo and (w < 1024 or 1))
+                nc.vector.quantize_mx(
+                    out=codes[:, lo:hi].bitcast(FP8X4), scales=scales[:, lo:hi], in_=flat[:, PACK * lo : PACK * hi]
+                )
+                lo = hi
+
+        def bring(item):
+            kind, a, s, n = item
+            if kind == "w1":
+                raw = rawp.tile([P, n, PACK, H], F32, name="raw")
+                rows = w1[a, s * K_PASS : (s + n) * K_PASS, :]
+                nc.sync.dma_start(raw[:], rows.rearrange("(g p j) c -> p g j c", p=P, j=PACK))
+                grouped = grp.tile([P, n, H * PACK], BF16, name="grouped", align_bytes=64)
+                dst = grouped[:].rearrange("p g (t m j) -> p g m t j", t=PACK, j=PACK)
+                src = raw[:].rearrange("p g j (m t) -> p g m t j", t=PACK)
+                cut = W1_VEC
+                flat = grouped[:].rearrange("p g f -> p (g f)")
+            elif kind == "w2":
+                raw = rawp.tile([P, n, PACK, N], F32, name="raw")
+                nc.sync.dma_start(raw[:], w2[a : a + n].rearrange("g (p j) n -> p g j n", j=PACK))
+                grouped = grp.tile([P, n, N, PACK], BF16, name="grouped", align_bytes=64)
+                dst = grouped[:]
+                src = raw[:].rearrange("p g j n -> p g n j")
+                cut = W2_VEC
+                flat = grouped[:].rearrange("p g n j -> p (g n j)")
+            else:
+                raw = rawp.tile([P, 1, PACK, T], F32, name="raw")
+                rows = xT[s * K_PASS : (s + 1) * K_PASS, :]
+                nc.sync.dma_start(raw[:, 0], rows.rearrange("(p j) n -> p j n", j=PACK))
+                grouped = grp.tile([P, 1, T, PACK], BF16, name="grouped", align_bytes=64)
+                dst = grouped[:]
+                src = raw[:].rearrange("p g j n -> p g n j")
+                cut = X_VEC
+                flat = grouped[:].rearrange("p g n j -> p (g n j)")
+            if n == 1:
+                dst, src = dst[:, 0], src[:, 0]
+                nc.scalar.copy(dst[:, cut:], src[:, cut:])
+                if cut:
+                    nc.vector.tensor_copy(dst[:, :cut], src[:, :cut])
+            else:
+                nc.scalar.copy(dst[:, :, cut:], src[:, :, cut:])
+                if cut:
+                    nc.vector.tensor_copy(dst[:, :, :cut], src[:, :, :cut])
+            return flat
+
+        def encode(item, flat):
+            kind, a, s, n = item
+            if kind == "x":
+                quantize(words[s], planes[4 * s : P, :], flat, T)
+                gather(words_g[s], words[s])
+                if s == PASSES - 1:
+                    gather(planes_g, planes)
+            elif kind == "w1":
+                codes = wcp.tile([P, n * H], U32, name="w1c", align_bytes=64)
+                scales = wcp.tile([P, n * H], U8, name="w1s", align_bytes=64)
+                quantize(codes, scales, flat, n * H)
+                for g in range(n):
+                    w1_codes[a, s + g] = (codes, scales, g * H)
+                if a == E - 1:
+                    if s == 0:
+                        accs[a] = [lastp.tile([P, C], F32, name="last%d" % t) for t in range(PACK)]
+                    for t in range(PACK):
+                        for g in range(n):
+                            layer1(accs[a][t][:], a, t, s + g)
+                elif s + n == PASSES:
+                    acc = accp.tile([P, PACK, C], F32, name="acc")
+                    accs[a] = acc
+                    for t in range(PACK):
+                        for q in range(PASSES):
+                            layer1(acc[:, t, :], a, t, q)
+            else:
+                codes = w2cp.tile([P, n * N], U32, name="w2c", align_bytes=64)
+                scales = w2cp.tile([P, n * N], U8, name="w2s", align_bytes=64)
+                quantize(codes, scales, flat, n * N)
+                for g in range(n):
+                    w2_codes[a + g] = (codes, scales, g * N)
+
+        def layer1(acc, e, t, s):
+            codes, scales, base = w1_codes[e, s]
+            cols = slice(base + t * P, base + (t + 1) * P)
+            nc.tensor.matmul_mx(
+                out=acc,
+                lhsT=codes[:, cols].bitcast(FP8X4),
+                lhsT_scale=scales[:, cols],
+                rhs=words_g[s][:, slots(e)].bitcast(FP8X4),
+                rhs_scale=planes_g[4 * s : P, slots(e)],
+                start=(s == 0),
+                stop=(s == PASSES - 1),
+            )
+
+        def activate(e, hb, part):
+            r = hp.tile([P, PACK, C], F32, name="r")
+            if e == E - 1:
+                for t in range(PACK):
+                    if t % 2 == 0:
+                        nc.scalar.activation(r[:, t, :], accs[e][t][:], RELU)
+                    else:
+                        nc.vector.tensor_scalar(r[:, t, :], accs[e][t][:], 0.0, None, MAX)
+            else:
+                nc.scalar.activation(r[:], accs[e][:], RELU)
+            nc.scalar.activation(hb[:, part], r[:].rearrange("p t c -> p c t"), SQUARE)
+
+        def layer2(group):
+            n = len(group)
+            hc = hp.tile([P, n * C], U32, name="hc", align_bytes=64)
+            hs = hp.tile([P, n * C], U8, name="hs", align_bytes=64)
+            quantize(hc, hs, hidden[group][:].rearrange("p g c t -> p (g c t)"), n * C)
+            gy = hp.tile([P, NB, n * C], F32, name="gy")
+            for part, e in enumerate(group):
+                y = yp.tile([P, NB, C], F32, name="y")
+                codes, scales, base = w2_codes[e]
+                for b in range(NB):
+                    cols = slice(base + b * P, base + (b + 1) * P)
+                    nc.tensor.matmul_mx(
+                        out=y[:, b, :],
+                        lhsT=codes[:, cols].bitcast(FP8X4),
+                        lhsT_scale=scales[:, cols],
+                        rhs=hc[:, slots(part)].bitcast(FP8X4),
+                        rhs_scale=hs[:, slots(part)],
+                        start=True,
+                        stop=True,
+                    )
+                nc.vector.tensor_tensor(gy[:, :, slots(part)], y[:], gate_t[:, :, slots(e)], MULT)
+            ys[group] = gy
+
+        def scatter(group, b):
+            lo, hi = group[0] * C // 16, (group[-1] + 1) * C // 16
+            nc.vector.tensor_copy(windows[b][:].indirect(offs_t[:, lo:hi]), ys[group][:, b, :])
+
+        items = [("x", 0, s, 1) for s in range(PASSES)]
+        for group in GROUPS:
+            for e in group:
+                n = 1 if e == E - 1 else 2
+                items += [("w1", e, s, n) for s in range(0, PASSES, n)]
+            items += [("w2", group[0], 0, len(group))]
+
+        later = {}
+
+        def plan(step, call):
+            later.setdefault(step, []).append(call)
+
+        flats = {}
+        step = 0
+        while step <= len(items) or any(k >= step for k in later):
+            if step < len(items):
+                flats[step] = bring(items[step])
+                if items[step][:3] == ("w1", 0, 2):
+                    nc.sync.dma_start(gate_t[:], gate.rearrange("(b p) s -> p b s", p=P))
+            if 0 < step <= len(items):
+                item = items[step - 1]
+                encode(item, flats[step - 1])
+                if item[0] == "w1" and item[2] + item[3] == PASSES:
+                    e = item[1]
+                    group = [g for g in GROUPS if e in g][0]
+                    if e == group[0]:
+                        hidden[group] = hp.tile([P, len(group), C, PACK], BF16, name="hb", align_bytes=64)
+                    plan(step + 1, lambda e=e, group=group: activate(e, hidden[group], e - group[0]))
+                    if e == group[-1]:
+                        plan(step + 2, lambda group=group: layer2(group))
+                        for b in range(NB):
+                            plan(step + 2 + b, lambda group=group, b=b: scatter(group, b))
+            for call in later.get(step, []):
+                call()
+            step += 1
+
+        for b in range(NB):
+            nc.sync.dma_start(out[b * P : (b + 1) * P, :], windows[b][:])

@@ -22,21 +22,21 @@ SQUARE = mybir.ActivationFunctionType.Square
 MULT = mybir.AluOpType.mult
 MAX = mybir.AluOpType.max
 
-X_VEC = 128
-W1_VEC = 32
-W2_VEC = 96
+X_VEC = 224
+W1_VEC = 52
+W2_VEC = 144
 HALF = SLOTS // 2
-GROUPS = [(0, 1), (2, 3), (4,), (5,)]
+GROUPS = [(e,) for e in range(E)]
 
 
 def tile_routed_moe_kernel(tc, xT, w1, w2, gate, offs, out):
     nc = tc.nc
     with ExitStack() as ctx:
         keep = ctx.enter_context(tc.tile_pool(name="keep", bufs=1))
-        rawp = ctx.enter_context(tc.tile_pool(name="rawp", bufs=6))
-        grp = ctx.enter_context(tc.tile_pool(name="grp", bufs=3))
-        wcp = ctx.enter_context(tc.tile_pool(name="wcp", bufs=6))
-        w2cp = ctx.enter_context(tc.tile_pool(name="w2cp", bufs=2))
+        rawp = ctx.enter_context(tc.tile_pool(name="rawp", bufs=9))
+        grp = ctx.enter_context(tc.tile_pool(name="grp", bufs=5))
+        wcp = ctx.enter_context(tc.tile_pool(name="wcp", bufs=10))
+        w2cp = ctx.enter_context(tc.tile_pool(name="w2cp", bufs=3))
         hp = ctx.enter_context(tc.tile_pool(name="hp", bufs=2))
         accp = ctx.enter_context(tc.psum_pool(name="accp", bufs=2))
         yp = ctx.enter_context(tc.psum_pool(name="yp", bufs=2))
@@ -80,26 +80,26 @@ def tile_routed_moe_kernel(tc, xT, w1, w2, gate, offs, out):
                 rows = w1[a, s * K_PASS : (s + n) * K_PASS, :]
                 nc.sync.dma_start(raw[:], rows.rearrange("(g p j) c -> p g j c", p=P, j=PACK))
                 grouped = grp.tile([P, n, H * PACK], BF16, name="grouped", align_bytes=64)
-                dst = grouped[:].rearrange("p g (t m j) -> p g m t j", t=PACK, j=PACK)
-                src = raw[:].rearrange("p g j (m t) -> p g m t j", t=PACK)
+                dst = grouped[:].rearrange("p g (t m j) -> p g m j t", t=PACK, j=PACK)
+                src = raw[:].rearrange("p g j (m t) -> p g m j t", t=PACK)
                 cut = W1_VEC
                 flat = grouped[:].rearrange("p g f -> p (g f)")
             elif kind == "w2":
                 raw = rawp.tile([P, n, PACK, N], F32, name="raw")
                 nc.sync.dma_start(raw[:], w2[a : a + n].rearrange("g (p j) n -> p g j n", j=PACK))
                 grouped = grp.tile([P, n, N, PACK], BF16, name="grouped", align_bytes=64)
-                dst = grouped[:]
-                src = raw[:].rearrange("p g j n -> p g n j")
-                cut = W2_VEC
+                dst = grouped[:].rearrange("p g (c i) j -> p g c j i", i=PACK)
+                src = raw[:].rearrange("p g j (c i) -> p g c j i", i=PACK)
+                cut = W2_VEC // PACK
                 flat = grouped[:].rearrange("p g n j -> p (g n j)")
             else:
                 raw = rawp.tile([P, 1, PACK, T], F32, name="raw")
                 rows = xT[s * K_PASS : (s + 1) * K_PASS, :]
                 nc.sync.dma_start(raw[:, 0], rows.rearrange("(p j) n -> p j n", j=PACK))
                 grouped = grp.tile([P, 1, T, PACK], BF16, name="grouped", align_bytes=64)
-                dst = grouped[:]
-                src = raw[:].rearrange("p g j n -> p g n j")
-                cut = X_VEC
+                dst = grouped[:].rearrange("p g (c i) j -> p g c j i", i=PACK)
+                src = raw[:].rearrange("p g j (c i) -> p g c j i", i=PACK)
+                cut = X_VEC // PACK
                 flat = grouped[:].rearrange("p g n j -> p (g n j)")
             if n == 1:
                 dst, src = dst[:, 0], src[:, 0]
@@ -197,11 +197,9 @@ def tile_routed_moe_kernel(tc, xT, w1, w2, gate, offs, out):
             nc.vector.tensor_copy(windows[b][:].indirect(offs_t[:, lo:hi]), ys[group][:, b, :])
 
         items = [("x", 0, s, 1) for s in range(PASSES)]
-        for group in GROUPS:
-            for e in group:
-                n = 1 if e == E - 1 else 2
-                items += [("w1", e, s, n) for s in range(0, PASSES, n)]
-            items += [("w2", group[0], 0, len(group))]
+        for e in range(E):
+            halves = [("w1", e, s, 1) for s in range(PASSES)]
+            items += halves + [("w2", e, 0, 1)] if e == E - 1 else [("w2", e, 0, 1)] + halves
 
         later = {}
 
@@ -213,7 +211,7 @@ def tile_routed_moe_kernel(tc, xT, w1, w2, gate, offs, out):
         while step <= len(items) or any(k >= step for k in later):
             if step < len(items):
                 flats[step] = bring(items[step])
-                if items[step][:3] == ("w1", 0, 2):
+                if items[step][:3] == ("w1", 0, PASSES - 1):
                     nc.sync.dma_start(gate_t[:], gate.rearrange("(b p) s -> p b s", p=P))
             if 0 < step <= len(items):
                 item = items[step - 1]

@@ -22,18 +22,19 @@ SQUARE = mybir.ActivationFunctionType.Square
 MULT = mybir.AluOpType.mult
 MAX = mybir.AluOpType.max
 
-X_VEC = 224
-W1_VEC = 52
-W2_VEC = 144
+X_VEC = 192
+W1_VEC = [128, 0, 128, 0]
+W1_VEC_LAST = 40
+W2_VEC = 0
 HALF = SLOTS // 2
-GROUPS = [(e,) for e in range(E)]
+RING = 8
 
 
 def tile_routed_moe_kernel(tc, xT, w1, w2, gate, offs, out):
     nc = tc.nc
     with ExitStack() as ctx:
         keep = ctx.enter_context(tc.tile_pool(name="keep", bufs=1))
-        rawp = ctx.enter_context(tc.tile_pool(name="rawp", bufs=9))
+        ring = ctx.enter_context(tc.tile_pool(name="ring", bufs=RING))
         grp = ctx.enter_context(tc.tile_pool(name="grp", bufs=5))
         wcp = ctx.enter_context(tc.tile_pool(name="wcp", bufs=10))
         w2cp = ctx.enter_context(tc.tile_pool(name="w2cp", bufs=3))
@@ -54,11 +55,9 @@ def tile_routed_moe_kernel(tc, xT, w1, w2, gate, offs, out):
         w1_codes = {}
         w2_codes = {}
         accs = {}
-        hidden = {}
-        ys = {}
 
-        def slots(e, n=1):
-            return slice(e * C, (e + n) * C)
+        def slots(e):
+            return slice(e * C, (e + 1) * C)
 
         def gather(dst, src):
             for lo in (0, HALF):
@@ -67,86 +66,83 @@ def tile_routed_moe_kernel(tc, xT, w1, w2, gate, offs, out):
         def quantize(codes, scales, flat, width):
             lo = 0
             while lo < width:
-                hi = lo + max(w for w in (1024, 512, 256, 128) if w <= width - lo and (w < 1024 or 1))
+                hi = lo + max(w for w in (512, 256, 128) if w <= width - lo)
                 nc.vector.quantize_mx(
                     out=codes[:, lo:hi].bitcast(FP8X4), scales=scales[:, lo:hi], in_=flat[:, PACK * lo : PACK * hi]
                 )
                 lo = hi
 
-        def bring(item):
-            kind, a, s, n = item
-            if kind == "w1":
-                raw = rawp.tile([P, n, PACK, H], F32, name="raw")
-                rows = w1[a, s * K_PASS : (s + n) * K_PASS, :]
-                nc.sync.dma_start(raw[:], rows.rearrange("(g p j) c -> p g j c", p=P, j=PACK))
-                grouped = grp.tile([P, n, H * PACK], BF16, name="grouped", align_bytes=64)
-                dst = grouped[:].rearrange("p g (t m j) -> p g m j t", t=PACK, j=PACK)
-                src = raw[:].rearrange("p g j (m t) -> p g m j t", t=PACK)
-                cut = W1_VEC
-                flat = grouped[:].rearrange("p g f -> p (g f)")
-            elif kind == "w2":
-                raw = rawp.tile([P, n, PACK, N], F32, name="raw")
-                nc.sync.dma_start(raw[:], w2[a : a + n].rearrange("g (p j) n -> p g j n", j=PACK))
-                grouped = grp.tile([P, n, N, PACK], BF16, name="grouped", align_bytes=64)
-                dst = grouped[:].rearrange("p g (c i) j -> p g c j i", i=PACK)
-                src = raw[:].rearrange("p g j (c i) -> p g c j i", i=PACK)
-                cut = W2_VEC // PACK
-                flat = grouped[:].rearrange("p g n j -> p (g n j)")
-            else:
-                raw = rawp.tile([P, 1, PACK, T], F32, name="raw")
-                rows = xT[s * K_PASS : (s + 1) * K_PASS, :]
-                nc.sync.dma_start(raw[:, 0], rows.rearrange("(p j) n -> p j n", j=PACK))
-                grouped = grp.tile([P, 1, T, PACK], BF16, name="grouped", align_bytes=64)
-                dst = grouped[:].rearrange("p g (c i) j -> p g c j i", i=PACK)
-                src = raw[:].rearrange("p g j (c i) -> p g c j i", i=PACK)
-                cut = X_VEC // PACK
-                flat = grouped[:].rearrange("p g n j -> p (g n j)")
-            if n == 1:
-                dst, src = dst[:, 0], src[:, 0]
-                nc.scalar.copy(dst[:, cut:], src[:, cut:])
-                if cut:
-                    nc.vector.tensor_copy(dst[:, :cut], src[:, :cut])
-            else:
-                nc.scalar.copy(dst[:, :, cut:], src[:, :, cut:])
-                if cut:
-                    nc.vector.tensor_copy(dst[:, :, :cut], src[:, :, :cut])
-            return flat
+        chunks = [("x", 0, s) for s in range(PASSES)]
+        for e in range(E - 1):
+            chunks += [("w1", e, s) for s in range(PASSES)] + [("w2", e, 0)]
+        chunks += [("w1", E - 1, s) for s in range(2)] + [("w2", E - 1, 0)] + [("w1", E - 1, s) for s in range(2, PASSES)]
+        relu_after = {chunks.index(("w1", e + 1, 1)): e for e in range(E - 1)}
+        raws = {}
 
-        def encode(item, flat):
-            kind, a, s, n = item
+        def load():
+            i = len(raws)
+            if i == len(chunks):
+                return
+            kind, e, s = chunks[i]
+            rows = slice(s * K_PASS, (s + 1) * K_PASS)
+            src = {"x": xT[rows, :], "w1": w1[e, rows, :], "w2": w2[e]}[kind]
+            raw = ring.tile([P, PACK, src.shape[1]], F32, name="raw")
+            nc.sync.dma_start(raw[:], src.rearrange("(p j) n -> p j n", j=PACK))
+            raws[i] = raw
+            if i == 7:
+                nc.sync.dma_start(gate_t[:], gate.rearrange("(b p) s -> p b s", p=P))
+
+        def interleave(i):
+            kind, e, s = chunks[i]
+            raw = raws[i]
+            width = raw.shape[2]
+            grouped = grp.tile([P, width * PACK], BF16, name="grouped", align_bytes=64)
+            if kind == "w1":
+                cut = W1_VEC_LAST if e == E - 1 else W1_VEC[s]
+                dst = grouped[:].rearrange("p (t m j) -> p m j t", t=PACK, j=PACK)
+                src = raw[:].rearrange("p j (m t) -> p m j t", t=PACK)
+            else:
+                cut = (X_VEC if kind == "x" else W2_VEC) // PACK
+                dst = grouped[:].rearrange("p (c i j) -> p c j i", i=PACK, j=PACK)
+                src = raw[:].rearrange("p j (c i) -> p c j i", i=PACK)
+            if cut < dst.shape[1]:
+                nc.scalar.copy(dst[:, cut:], src[:, cut:])
+            if cut > 0:
+                nc.vector.tensor_copy(dst[:, :cut], src[:, :cut])
+            return grouped
+
+        def encode(i, grouped):
+            kind, e, s = chunks[i]
             if kind == "x":
-                quantize(words[s], planes[4 * s : P, :], flat, T)
+                quantize(words[s], planes[4 * s : P, :], grouped[:], T)
                 gather(words_g[s], words[s])
                 if s == PASSES - 1:
                     gather(planes_g, planes)
             elif kind == "w1":
-                codes = wcp.tile([P, n * H], U32, name="w1c", align_bytes=64)
-                scales = wcp.tile([P, n * H], U8, name="w1s", align_bytes=64)
-                quantize(codes, scales, flat, n * H)
-                for g in range(n):
-                    w1_codes[a, s + g] = (codes, scales, g * H)
-                if a == E - 1:
+                codes = wcp.tile([P, H], U32, name="w1c", align_bytes=64)
+                scales = wcp.tile([P, H], U8, name="w1s", align_bytes=64)
+                quantize(codes, scales, grouped[:], H)
+                w1_codes[e, s] = (codes, scales)
+                if e == E - 1:
                     if s == 0:
-                        accs[a] = [lastp.tile([P, C], F32, name="last%d" % t) for t in range(PACK)]
+                        accs[e] = [lastp.tile([P, C], F32, name="last%d" % t) for t in range(PACK)]
                     for t in range(PACK):
-                        for g in range(n):
-                            layer1(accs[a][t][:], a, t, s + g)
-                elif s + n == PASSES:
+                        layer1(accs[e][t][:], e, t, s)
+                elif s == PASSES - 1:
                     acc = accp.tile([P, PACK, C], F32, name="acc")
-                    accs[a] = acc
+                    accs[e] = acc
                     for t in range(PACK):
                         for q in range(PASSES):
-                            layer1(acc[:, t, :], a, t, q)
+                            layer1(acc[:, t, :], e, t, q)
             else:
-                codes = w2cp.tile([P, n * N], U32, name="w2c", align_bytes=64)
-                scales = w2cp.tile([P, n * N], U8, name="w2s", align_bytes=64)
-                quantize(codes, scales, flat, n * N)
-                for g in range(n):
-                    w2_codes[a + g] = (codes, scales, g * N)
+                codes = w2cp.tile([P, N], U32, name="w2c", align_bytes=64)
+                scales = w2cp.tile([P, N], U8, name="w2s", align_bytes=64)
+                quantize(codes, scales, grouped[:], N)
+                w2_codes[e] = (codes, scales)
 
         def layer1(acc, e, t, s):
-            codes, scales, base = w1_codes[e, s]
-            cols = slice(base + t * P, base + (t + 1) * P)
+            codes, scales = w1_codes[e, s]
+            cols = slice(t * P, (t + 1) * P)
             nc.tensor.matmul_mx(
                 out=acc,
                 lhsT=codes[:, cols].bitcast(FP8X4),
@@ -157,78 +153,47 @@ def tile_routed_moe_kernel(tc, xT, w1, w2, gate, offs, out):
                 stop=(s == PASSES - 1),
             )
 
-        def activate(e, hb, part):
-            r = hp.tile([P, PACK, C], F32, name="r")
+        def layer2(e):
+            hb = hp.tile([P, C, PACK], BF16, name="hb", align_bytes=64)
             if e == E - 1:
+                r = keep.tile([P, PACK, C], F32, name="r_last")
                 for t in range(PACK):
                     if t % 2 == 0:
                         nc.scalar.activation(r[:, t, :], accs[e][t][:], RELU)
                     else:
                         nc.vector.tensor_scalar(r[:, t, :], accs[e][t][:], 0.0, None, MAX)
             else:
+                r = ring.tile([P, PACK, C], F32, name="raw")
                 nc.scalar.activation(r[:], accs[e][:], RELU)
-            nc.scalar.activation(hb[:, part], r[:].rearrange("p t c -> p c t"), SQUARE)
+            nc.scalar.activation(hb[:], r[:].rearrange("p t c -> p c t"), SQUARE)
+            hc = hp.tile([P, C], U32, name="hc", align_bytes=64)
+            hs = hp.tile([P, C], U8, name="hs", align_bytes=64)
+            quantize(hc, hs, hb[:].rearrange("p c t -> p (c t)"), C)
+            y = yp.tile([P, NB, C], F32, name="y")
+            gy = hp.tile([P, NB, C], F32, name="gy")
+            codes, scales = w2_codes[e]
+            for b in range(NB):
+                cols = slice(b * P, (b + 1) * P)
+                nc.tensor.matmul_mx(
+                    out=y[:, b, :],
+                    lhsT=codes[:, cols].bitcast(FP8X4),
+                    lhsT_scale=scales[:, cols],
+                    rhs=hc[:].bitcast(FP8X4),
+                    rhs_scale=hs[:],
+                    start=True,
+                    stop=True,
+                )
+            nc.vector.tensor_tensor(gy[:], y[:], gate_t[:, :, slots(e)], MULT)
+            for b in range(NB):
+                nc.vector.tensor_copy(windows[b][:].indirect(offs_t[:, e * C // 16 : (e + 1) * C // 16]), gy[:, b, :])
 
-        def layer2(group):
-            n = len(group)
-            hc = hp.tile([P, n * C], U32, name="hc", align_bytes=64)
-            hs = hp.tile([P, n * C], U8, name="hs", align_bytes=64)
-            quantize(hc, hs, hidden[group][:].rearrange("p g c t -> p (g c t)"), n * C)
-            gy = hp.tile([P, NB, n * C], F32, name="gy")
-            for part, e in enumerate(group):
-                y = yp.tile([P, NB, C], F32, name="y")
-                codes, scales, base = w2_codes[e]
-                for b in range(NB):
-                    cols = slice(base + b * P, base + (b + 1) * P)
-                    nc.tensor.matmul_mx(
-                        out=y[:, b, :],
-                        lhsT=codes[:, cols].bitcast(FP8X4),
-                        lhsT_scale=scales[:, cols],
-                        rhs=hc[:, slots(part)].bitcast(FP8X4),
-                        rhs_scale=hs[:, slots(part)],
-                        start=True,
-                        stop=True,
-                    )
-                nc.vector.tensor_tensor(gy[:, :, slots(part)], y[:], gate_t[:, :, slots(e)], MULT)
-            ys[group] = gy
-
-        def scatter(group, b):
-            lo, hi = group[0] * C // 16, (group[-1] + 1) * C // 16
-            nc.vector.tensor_copy(windows[b][:].indirect(offs_t[:, lo:hi]), ys[group][:, b, :])
-
-        items = [("x", 0, s, 1) for s in range(PASSES)]
-        for e in range(E):
-            halves = [("w1", e, s, 1) for s in range(PASSES)]
-            items += halves + [("w2", e, 0, 1)] if e == E - 1 else [("w2", e, 0, 1)] + halves
-
-        later = {}
-
-        def plan(step, call):
-            later.setdefault(step, []).append(call)
-
-        flats = {}
-        step = 0
-        while step <= len(items) or any(k >= step for k in later):
-            if step < len(items):
-                flats[step] = bring(items[step])
-                if items[step][:3] == ("w1", 0, PASSES - 1):
-                    nc.sync.dma_start(gate_t[:], gate.rearrange("(b p) s -> p b s", p=P))
-            if 0 < step <= len(items):
-                item = items[step - 1]
-                encode(item, flats[step - 1])
-                if item[0] == "w1" and item[2] + item[3] == PASSES:
-                    e = item[1]
-                    group = [g for g in GROUPS if e in g][0]
-                    if e == group[0]:
-                        hidden[group] = hp.tile([P, len(group), C, PACK], BF16, name="hb", align_bytes=64)
-                    plan(step + 1, lambda e=e, group=group: activate(e, hidden[group], e - group[0]))
-                    if e == group[-1]:
-                        plan(step + 2, lambda group=group: layer2(group))
-                        for b in range(NB):
-                            plan(step + 2 + b, lambda group=group, b=b: scatter(group, b))
-            for call in later.get(step, []):
-                call()
-            step += 1
-
+        for i in range(RING):
+            load()
+        for i in range(len(chunks)):
+            encode(i, interleave(i))
+            if i in relu_after:
+                layer2(relu_after[i])
+            load()
+        layer2(E - 1)
         for b in range(NB):
             nc.sync.dma_start(out[b * P : (b + 1) * P, :], windows[b][:])

@@ -22,9 +22,9 @@ SQUARE = mybir.ActivationFunctionType.Square
 MULT = mybir.AluOpType.mult
 MAX = mybir.AluOpType.max
 
-X_VEC = 192
-W1_VEC = [128, 0, 128, 0]
-W1_VEC_LAST = 40
+X_VEC = 160
+W1_VEC = [32, 128, 96, 0]
+W1_VEC_LAST = 44
 W2_VEC = 0
 HALF = SLOTS // 2
 RING = 8
@@ -39,7 +39,6 @@ def tile_routed_moe_kernel(tc, xT, w1, w2, gate, offs, out):
         wcp = ctx.enter_context(tc.tile_pool(name="wcp", bufs=10))
         w2cp = ctx.enter_context(tc.tile_pool(name="w2cp", bufs=3))
         hp = ctx.enter_context(tc.tile_pool(name="hp", bufs=2))
-        accp = ctx.enter_context(tc.psum_pool(name="accp", bufs=2))
         yp = ctx.enter_context(tc.psum_pool(name="yp", bufs=2))
         lastp = ctx.enter_context(tc.psum_pool(name="lastp", bufs=1))
 
@@ -74,9 +73,9 @@ def tile_routed_moe_kernel(tc, xT, w1, w2, gate, offs, out):
 
         chunks = [("x", 0, s) for s in range(PASSES)]
         for e in range(E - 1):
-            chunks += [("w1", e, s) for s in range(PASSES)] + [("w2", e, 0)]
-        chunks += [("w1", E - 1, s) for s in range(2)] + [("w2", E - 1, 0)] + [("w1", E - 1, s) for s in range(2, PASSES)]
-        relu_after = {chunks.index(("w1", e + 1, 1)): e for e in range(E - 1)}
+            chunks += [("w1", e, 0), ("w1", e, 1), ("w2", e, 0), ("w1", e, 2), ("w1", e, 3)]
+        chunks += [("w1", E - 1, s) for s in range(4)] + [("w2", E - 1, 0)] + [("w1", E - 1, s) for s in range(4, PASSES)]
+        relu_after = {chunks.index(("w1", e + 1, 0)): e for e in range(E - 1)}
         raws = {}
 
         def load():
@@ -123,17 +122,10 @@ def tile_routed_moe_kernel(tc, xT, w1, w2, gate, offs, out):
                 scales = wcp.tile([P, H], U8, name="w1s", align_bytes=64)
                 quantize(codes, scales, grouped[:], H)
                 w1_codes[e, s] = (codes, scales)
-                if e == E - 1:
-                    if s == 0:
-                        accs[e] = [lastp.tile([P, C], F32, name="last%d" % t) for t in range(PACK)]
-                    for t in range(PACK):
-                        layer1(accs[e][t][:], e, t, s)
-                elif s == PASSES - 1:
-                    acc = accp.tile([P, PACK, C], F32, name="acc")
-                    accs[e] = acc
-                    for t in range(PACK):
-                        for q in range(PASSES):
-                            layer1(acc[:, t, :], e, t, q)
+                if s == 0:
+                    accs[e] = [lastp.tile([P, C], F32, name="last%d" % t) for t in range(PACK)]
+                for t in range(PACK):
+                    layer1(accs[e][t][:], e, t, s)
             else:
                 codes = w2cp.tile([P, N], U32, name="w2c", align_bytes=64)
                 scales = w2cp.tile([P, N], U8, name="w2s", align_bytes=64)
@@ -155,16 +147,12 @@ def tile_routed_moe_kernel(tc, xT, w1, w2, gate, offs, out):
 
         def layer2(e):
             hb = hp.tile([P, C, PACK], BF16, name="hb", align_bytes=64)
-            if e == E - 1:
-                r = keep.tile([P, PACK, C], F32, name="r_last")
-                for t in range(PACK):
-                    if t % 2 == 0:
-                        nc.scalar.activation(r[:, t, :], accs[e][t][:], RELU)
-                    else:
-                        nc.vector.tensor_scalar(r[:, t, :], accs[e][t][:], 0.0, None, MAX)
-            else:
-                r = ring.tile([P, PACK, C], F32, name="raw")
-                nc.scalar.activation(r[:], accs[e][:], RELU)
+            r = hp.tile([P, PACK, C], F32, name="r")
+            for t in range(PACK):
+                if e < E - 1 or t % 2 == 0:
+                    nc.scalar.activation(r[:, t, :], accs[e][t][:], RELU)
+                else:
+                    nc.vector.tensor_scalar(r[:, t, :], accs[e][t][:], 0.0, None, MAX)
             nc.scalar.activation(hb[:], r[:].rearrange("p t c -> p c t"), SQUARE)
             hc = hp.tile([P, C], U32, name="hc", align_bytes=64)
             hs = hp.tile([P, C], U8, name="hs", align_bytes=64)

from contextlib import ExitStack

import concourse.mybir as mybir

K, T, E, C, H, N = 2048, 768, 6, 128, 512, 384
P = 128
PACK = 4
K_PASS = P * PACK
PASSES = K // K_PASS
NB = N // P
SLOTS = E * C
FLOPS = 2 * SLOTS * (K * H + H * N)

F32 = mybir.dt.float32
BF16 = mybir.dt.bfloat16
U32 = mybir.dt.uint32
U16 = mybir.dt.uint16
U8 = mybir.dt.uint8
FP8X4 = mybir.dt.float8_e4m3fn_x4
RELU = mybir.ActivationFunctionType.Relu
SQUARE = mybir.ActivationFunctionType.Square
MULT = mybir.AluOpType.mult
MAX = mybir.AluOpType.max

X_VEC = 160
W1_VEC = [32, 128, 96, 0]
W1_VEC_LAST = 44
W2_VEC = 0
HALF = SLOTS // 2
RING = 8


def tile_routed_moe_kernel(tc, xT, w1, w2, gate, offs, out):
    nc = tc.nc
    with ExitStack() as ctx:
        keep = ctx.enter_context(tc.tile_pool(name="keep", bufs=1))
        ring = ctx.enter_context(tc.tile_pool(name="ring", bufs=RING))
        grp = ctx.enter_context(tc.tile_pool(name="grp", bufs=5))
        wcp = ctx.enter_context(tc.tile_pool(name="wcp", bufs=10))
        w2cp = ctx.enter_context(tc.tile_pool(name="w2cp", bufs=3))
        hp = ctx.enter_context(tc.tile_pool(name="hp", bufs=2))
        yp = ctx.enter_context(tc.psum_pool(name="yp", bufs=2))
        lastp = ctx.enter_context(tc.psum_pool(name="lastp", bufs=1))

        offs_t = keep.tile([P, SLOTS // 16], U16, name="offs_t")
        nc.sync.dma_start(offs_t[:], offs)
        planes = keep.tile([P, T], U8, name="planes", align_bytes=64)
        nc.gpsimd.memset(planes[:], 0)
        planes_g = keep.tile([P, SLOTS], U8, name="planes_g", align_bytes=64)
        gate_t = keep.tile([P, NB, SLOTS], F32, name="gate_t")
        windows = [keep.tile([P, T], F32, name="window%d" % b) for b in range(NB)]
        words = [keep.tile([P, T], U32, name="words%d" % s, align_bytes=64) for s in range(PASSES)]
        words_g = [keep.tile([P, SLOTS], U32, name="words_g%d" % s, align_bytes=64) for s in range(PASSES)]
        w1_codes = {}
        w2_codes = {}
        accs = {}

        def slots(e):
            return slice(e * C, (e + 1) * C)

        def gather(dst, src):
            for lo in (0, HALF):
                nc.vector.tensor_copy(dst[:, lo : lo + HALF], src[:].indirect(offs_t[:, lo // 16 : (lo + HALF) // 16]))

        def quantize(codes, scales, flat, width):
            lo = 0
            while lo < width:
                hi = lo + max(w for w in (512, 256, 128) if w <= width - lo)
                nc.vector.quantize_mx(
                    out=codes[:, lo:hi].bitcast(FP8X4), scales=scales[:, lo:hi], in_=flat[:, PACK * lo : PACK * hi]
                )
                lo = hi

        chunks = [("x", 0, s) for s in range(PASSES)]
        for e in range(E - 1):
            chunks += [("w1", e, 0), ("w1", e, 1), ("w2", e, 0), ("w1", e, 2), ("w1", e, 3)]
        chunks += [("w1", E - 1, s) for s in range(4)] + [("w2", E - 1, 0)] + [("w1", E - 1, s) for s in range(4, PASSES)]
        relu_after = {chunks.index(("w1", e + 1, 0)): e for e in range(E - 1)}
        raws = {}

        def load():
            i = len(raws)
            if i == len(chunks):
                return
            kind, e, s = chunks[i]
            rows = slice(s * K_PASS, (s + 1) * K_PASS)
            src = {"x": xT[rows, :], "w1": w1[e, rows, :], "w2": w2[e]}[kind]
            raw = ring.tile([P, PACK, src.shape[1]], F32, name="raw")
            nc.sync.dma_start(raw[:], src.rearrange("(p j) n -> p j n", j=PACK))
            raws[i] = raw
            if i == 7:
                nc.sync.dma_start(gate_t[:], gate.rearrange("(b p) s -> p b s", p=P))

        def interleave(i):
            kind, e, s = chunks[i]
            raw = raws[i]
            width = raw.shape[2]
            grouped = grp.tile([P, width * PACK], BF16, name="grouped", align_bytes=64)
            if kind == "w1":
                cut = W1_VEC_LAST if e == E - 1 else W1_VEC[s]
                dst = grouped[:].rearrange("p (t m j) -> p m j t", t=PACK, j=PACK)
                src = raw[:].rearrange("p j (m t) -> p m j t", t=PACK)
            else:
                cut = (X_VEC if kind == "x" else W2_VEC) // PACK
                dst = grouped[:].rearrange("p (c i j) -> p c j i", i=PACK, j=PACK)
                src = raw[:].rearrange("p j (c i) -> p c j i", i=PACK)
            if cut < dst.shape[1]:
                nc.scalar.copy(dst[:, cut:], src[:, cut:])
            if cut > 0:
                nc.vector.tensor_copy(dst[:, :cut], src[:, :cut])
            return grouped

        def encode(i, grouped):
            kind, e, s = chunks[i]
            if kind == "x":
                quantize(words[s], planes[4 * s : P, :], grouped[:], T)
                gather(words_g[s], words[s])
                if s == PASSES - 1:
                    gather(planes_g, planes)
            elif kind == "w1":
                codes = wcp.tile([P, H], U32, name="w1c", align_bytes=64)
                scales = wcp.tile([P, H], U8, name="w1s", align_bytes=64)
                quantize(codes, scales, grouped[:], H)
                w1_codes[e, s] = (codes, scales)
                if s == 0:
                    accs[e] = [lastp.tile([P, C], F32, name="last%d" % t) for t in range(PACK)]
                for t in range(PACK):
                    layer1(accs[e][t][:], e, t, s)
            else:
                codes = w2cp.tile([P, N], U32, name="w2c", align_bytes=64)
                scales = w2cp.tile([P, N], U8, name="w2s", align_bytes=64)
                quantize(codes, scales, grouped[:], N)
                w2_codes[e] = (codes, scales)

        def layer1(acc, e, t, s):
            codes, scales = w1_codes[e, s]
            cols = slice(t * P, (t + 1) * P)
            nc.tensor.matmul_mx(
                out=acc,
                lhsT=codes[:, cols].bitcast(FP8X4),
                lhsT_scale=scales[:, cols],
                rhs=words_g[s][:, slots(e)].bitcast(FP8X4),
                rhs_scale=planes_g[4 * s : P, slots(e)],
                start=(s == 0),
                stop=(s == PASSES - 1),
            )

        def layer2(e):
            hb = hp.tile([P, C, PACK], BF16, name="hb", align_bytes=64)
            r = hp.tile([P, PACK, C], F32, name="r")
            for t in range(PACK):
                if e < E - 1 or t % 2 == 0:
                    nc.scalar.activation(r[:, t, :], accs[e][t][:], RELU)
                else:
                    nc.vector.tensor_scalar(r[:, t, :], accs[e][t][:], 0.0, None, MAX)
            nc.scalar.activation(hb[:], r[:].rearrange("p t c -> p c t"), SQUARE)
            hc = hp.tile([P, C], U32, name="hc", align_bytes=64)
            hs = hp.tile([P, C], U8, name="hs", align_bytes=64)
            quantize(hc, hs, hb[:].rearrange("p c t -> p (c t)"), C)
            y = yp.tile([P, NB, C], F32, name="y")
            gy = hp.tile([P, NB, C], F32, name="gy")
            codes, scales = w2_codes[e]
            for b in range(NB):
                cols = slice(b * P, (b + 1) * P)
                nc.tensor.matmul_mx(
                    out=y[:, b, :],
                    lhsT=codes[:, cols].bitcast(FP8X4),
                    lhsT_scale=scales[:, cols],
                    rhs=hc[:].bitcast(FP8X4),
                    rhs_scale=hs[:],
                    start=True,
                    stop=True,
                )
            nc.vector.tensor_tensor(gy[:], y[:], gate_t[:, :, slots(e)], MULT)
            for b in range(NB):
                nc.vector.tensor_copy(windows[b][:].indirect(offs_t[:, e * C // 16 : (e + 1) * C // 16]), gy[:, b, :])

        for i in range(RING):
            load()
        for i in range(len(chunks)):
            encode(i, interleave(i))
            if i in relu_after:
                layer2(relu_after[i])
            load()
        layer2(E - 1)
        for b in range(NB):
            nc.sync.dma_start(out[b * P : (b + 1) * P, :], windows[b][:])
